import numpy as np, ml_dtypes
CORES = [2,6,10,14,18,22,26,30]
N = 8
BF = ml_dtypes.bfloat16
M, L, KH, CAP, RO, OC = 4096, 256, 10, 32, 3, 4096
S = 16
def pack(b, o, w):
    return {"ball": np.ascontiguousarray(b.reshape(N, 128, M)).astype(np.float32).astype(BF), "stk": np.ascontiguousarray(o.reshape(N, 128, L)).astype(np.int32),
            "wt": np.ascontiguousarray(w.reshape(N, 128, 1)).astype(np.float32).astype(BF)}
def halves(rng):
    bright = np.argsort(rng.random((N, 8, M)), axis=-1) < M // 2
    return np.where(bright[:, :, None], rng.integers(140, 256, (N, 8, 16, M)), rng.integers(0, 120, (N, 8, 16, M))), bright
def stacks(rng, kk, bright):
    br, di = np.flatnonzero(bright), np.flatnonzero(~bright); dep = np.arange(16)[:, None]
    o = rng.integers(0, M, (16, L)); top = np.where(kk > 0, rng.choice(br, L), rng.choice(di, L))
    o = np.where((dep > 0) & (dep <= kk), rng.choice(di, (16, L)), o)
    o = np.where(dep == kk + 1, np.where(kk > 0, top, rng.choice(br, L)), o)
    o[0] = top
    return o
def later(rng, z):
    kk = np.concatenate([np.full(L // 2, 15), np.zeros(z, np.int64), rng.integers(1, KH, L - L // 2 - z)])
    kk[:int(np.sum(kk)) % S] = 14
    kk = rng.permutation(kk); dep = np.arange(16)[:, None]
    kind = rng.permutation(np.arange(M - L) % 3)
    b = rng.integers(0, 256, (16, M))
    b[:, L:] = np.where(kind == 0, rng.integers(0, 40, (16, M - L)), np.where(kind == 1, rng.integers(60, 200, (16, M - L)), 255))
    low, mid, top = L + np.flatnonzero(kind == 0), L + np.flatnonzero(kind == 1), L + np.flatnonzero(kind == 2)
    o = np.where((dep > 0) & (dep <= kk), rng.choice(mid, (16, L)), rng.integers(0, M, (16, L)))
    o = np.where(dep == kk + 1, rng.choice(top, (16, L)), o)
    o[0] = rng.choice(low, L)
    return b, o
def quiet(rng, a):
    c = np.arange(M) // L; free = rng.permutation(np.flatnonzero((c > 0) & (c != a)))
    low, top = free[:16], free[16:M // 2]
    b = rng.integers(0, 256, (16, M)); b[:, low] = 0; b[:, top] = 255
    o = rng.integers(0, M, (16, L)); one = rng.permutation(L) < a
    o[0] = np.where(one, rng.choice(top, L), o[0]); o[1] = np.where(one, rng.choice(low, L), rng.choice(top, L)); o[2] = np.where(one, rng.choice(top, L), o[2])
    return b, o
def setup_inputs(rng):
    lev = rng.integers(0, 256, (N, 8, 1, M))
    b = np.clip(lev + np.rint(24 * rng.standard_normal((N, 8, 16, M), dtype=np.float32)).astype(np.int64), 0, 255)
    o = rng.integers(0, M, (N, 8, 16, L)); high = np.argsort(lev[:, :, 0], axis=-1)[..., M - M // 8:]
    pick = np.take_along_axis(high, rng.integers(0, M // 8, (N, 8, L)), 2); share = rng.choice(np.array([0.0, 0.1, 0.3, 0.5]), (N, 8, 1))
    o[:, :, 0] = np.where(rng.random((N, 8, L)) < share, pick, o[:, :, 0])
    return pack(b, o, rng.integers(0, 256, (N, 8, 16, 1)))
def setup_inputs_room(rng):
    b, bright = halves(rng); o = np.zeros((N, 8, 16, L), np.int64); c = np.array([0, 1, CAP - 1, CAP, CAP + 1, L])
    for q in range(N):
        for g in range(8):
            n, z = int(rng.choice(c)), int(rng.choice(c))
            if q in (0, 2): n = (CAP, CAP + 1, L, CAP - 1, 1, 0, CAP, CAP + 1)[g]
            if q in (1, 3):
                z = (CAP, CAP + 1, CAP, CAP, 0, L, CAP - 1, 1)[g]; n = min(n, L - z)
            z = min(z, L - n)
            kk = np.concatenate([rng.choice(np.array([KH, KH, KH + 1, 15]), n), np.zeros(z, np.int64), rng.choice(np.array([1, KH // 2, KH - 1, KH - 1]), L - n - z)])
            kk = rng.permutation(kk)
            if q in (0, 2) and g == 0:
                i = int(np.flatnonzero(kk >= KH)[0]); kk[[i, L - 1]] = kk[[L - 1, i]]
            if q in (1, 3) and g < 3: kk = kk[np.argsort(kk > 0, kind="stable")]
            o[q, g] = stacks(rng, kk, bright[q, g])
    return pack(b, o, rng.integers(0, 256, (N, 8, 16, 1)))
def setup_inputs_votes(rng):
    base = rng.integers(1, 255, (N, 8, 16, 1)); j = rng.choice(np.array([7, 8, 9, 10, 16]), (N, 8, 1, M), p=[0.04, 0.06, 0.5, 0.2, 0.2])
    place = np.argsort(rng.random((N, 8, 16, M)), axis=2)
    b = base - (place < j) + (place >= j) * rng.integers(0, 2, (N, 8, 16, M))
    b[..., ::4] = base
    o = 4 * rng.integers(0, M // 4, (N, 8, 16, L)) + rng.integers(1, 4, (N, 8, 16, L))
    o[:, :, 0] = np.where(rng.random((N, 8, L)) < 0.7, 4 * rng.integers(0, M // 4, (N, 8, L)), o[:, :, 0])
    return pack(b, o, rng.integers(0, 256, (N, 8, 16, 1)))
def setup_inputs_ends(rng):
    b, bright = halves(rng); b[..., 0] = 255; b[..., M - 1] = 0; bright[..., 0] = True; bright[..., M - 1] = False
    b[:, 4, :, 1023] = 255; b[:, 4, :, M - 16] = 0; bright[:, 4, 1023] = True; bright[:, 4, M - 16] = False
    o = np.zeros((N, 8, 16, L), np.int64); w = rng.integers(0, 256, (N, 8, 16, 1)); w[:, 0::2] = 255; w[:, 1] = 0; w[:, 5:] = 0
    for q in range(N):
        for g in range(8):
            kk = rng.integers(0, 16, L); kk[0] = 15 * (q % 2); kk[L - 1] = 15 * (1 - q % 2)
            if g == 4: kk[:] = 15
            if g == 6: b[q, g], o[q, g] = quiet(rng, int(rng.integers(1, S)))
            elif g in (5, 7): b[q, g], o[q, g] = later(rng, (0, 1, CAP // 2, CAP - 1)[(q + g) % 4])
            else: o[q, g] = stacks(rng, kk, bright[q, g])
    o[:, 0] = rng.choice(np.array([M - 1, M - 1, M - 1, M - 1, M - 1, M - 1, 0]), (N, 16, L))
    o[:, 0, 0] = rng.choice(np.array([0, 0, M - 1]), (N, L))
    o[:, 2] = o[:, 2, :1]
    far = np.where(np.arange(16)[:, None] == 0, 1023, rng.choice(np.array([M - 1, M - 16]), (N, 16, L)))
    o[:, 4] = np.where(rng.random((N, 1, L)) < 0.25, far, o[:, 4])
    return pack(b, o, w)
def setup_inputs_spread(rng):
    b = np.minimum(np.exp2(8.5 * rng.random((N, 8, 1, M))) * rng.random((N, 8, 16, M)), 255.0).astype(np.int64) * (rng.random((N, 8, 1, M)) > 0.0625)
    w = np.exp2(8 * rng.random((N, 8, 16, 1))).astype(np.int64) - 1
    o = (M * rng.random((N, 8, 16, L)) ** rng.choice(np.array([1, 2, 4]), (N, 8, 1, 1))).astype(np.int64)
    return pack(b, o, w)
def check_inputs(d):
    bad = []
    for k, hi in (("ball", 255), ("stk", M - 1), ("wt", 255)):
        v = np.asarray(d[k]).astype(np.float64)
        if not (np.min(v) >= 0 and np.max(v) <= hi): bad.append("range of " + k)
        elif np.any(v != np.floor(v)): bad.append("whole numbers in " + k)
    return bad
def reference(ball, stk, wt):
    b = ball.astype(np.float32).astype(np.int64).reshape(N, 8, 16, M)
    o = stk.astype(np.int64).reshape(N, 8, 16, L)
    w = wt.astype(np.float32).astype(np.int64).reshape(N, 8, 16, 1)
    lane = np.arange(L); dep = np.arange(16)[:, None]
    for t in range(RO):
        p = np.take_along_axis(b, o.reshape(N, 8, 1, 16 * L), 3).reshape(N, 8, 16, 16, L)
        x, rest = p[:, :, :, 0], p[:, :, :, 1:]
        won = np.add.reduce((x[:, :, :, None] > rest).astype(np.int64), axis=2) >= 9
        crossed = np.multiply.accumulate(won.astype(np.int64), axis=2)
        k = np.add.reduce(crossed, axis=2)
        top = np.where(k[:, :, None] == 0, 255, np.max(rest * crossed[:, :, None], axis=3))
        y = np.abs(x - top)
        A = np.add.reduce(k, axis=2)
        v = L * ((np.add.reduce(w * y, axis=2) + A[:, :, None]) & (S - 1)) + lane
        new = (((o * (2 * (o[:, :, :1] & 1023) + 1)) >> 4) + A[:, :, None, None]) & (M - 1)
        up = np.concatenate([new[:, :, 1:], new[:, :, :1]], axis=2)
        o = np.where(dep < k[:, :, None], up, np.where(dep == k[:, :, None], v[:, :, None], o))
        z = y.copy()
        for r in range(N):
            q = (r - 1 - t) % N
            for g in range(8):
                src = np.flatnonzero(k[q, g] >= KH)[:CAP]; dst = np.flatnonzero(k[r, g] == 0)[:len(src)]
                z[r, g][:, dst] = y[q, g][:, src[:len(dst)]]
        np.put_along_axis(b, v[:, :, None, :], z, 3)
    return {"yo": o.reshape(N, 128, L).astype(np.float32), "yb": b.reshape(N, 128, M)[:, :, :OC].astype(np.float32).astype(BF)}

@@ -1,0 +1,335 @@
+import numpy as np
+from concourse.mybir import AluOpType, AxisListType, ActivationFunctionType
+
+OP = AluOpType
+AF = ActivationFunctionType
+ROUNDS = 3
+NB = 4096
+DUMP = 32
+CH = 4
+CW = NB // CH
+
+SCRATCH = {}
+
+
+def _declare(where, dtype, **shapes):
+    for name, n in shapes.items():
+        SCRATCH[name] = (where, [128] + (n if isinstance(n, list) else [n]), dtype)
+
+
+_declare("sbuf", "bfloat16", B=NB + DUMP, P=NB, PM=NB, WN=[16, 256], tw=256, st=256, K=256, D=272, Y=256, HF=256, ZF=256,
+         CZ=256, J=256, C=256, EK=256, ob=256, ID=128, B1=128, BO=128, WB=128, E1=144, E2=144, E01=144, WE=144, RS=CW,
+         KS=256, KT=16, iL=16, row=256, wb=1,
+         CH0=256, CH1=256, CH2=256, PK0=32, PK1=32, PK2=32, RX0=32, RX1=32, RX2=32, RC0=1, RC1=1, RC2=1)
+_declare("sbuf", "float32", S16=256, kb=16, A16=1, A4=1, acch=2, accz=2, vraw=272, G32=32, GM=32, rd=2, mn=1, nk=2, nd=2,
+         of=2, ef=256, zu=256, t3=256, yof=256, of32=128, c16=128, cm1=128, LE=128, LS=128, NI=128, rc=1, d16=1, bs=2,
+         nc=2, dm=2, j16=16, iF=16, KB=16, rowf=256, cm=32, DM=32, wf=1)
+_declare("sbuf", "int32", SI=256, eI=256, UI=256, VI=16, VB=16, ri=2, rb=2, pI=1, rI=1, wI=1, wA=1)
+_declare("sbuf", "uint16", SU=256, kl0=16, kl1=16, hl=2, zl=2, OL=2, VL=16)
+_declare("psum", "float32", psX0=512, psX1=512, psV=512, psE=512, psD=512, psS=512, psR=512, psL=512)
+
+DMAS = ["in_stk", "in_wt", "in_ball", "out_yo", "out_yb"]
+SEMAPHORES = (["qv", "qs", "qt", "qg", "ls"] + ["dma_" + d for d in DMAS]
+              + ["cnt%d" % t for t in range(ROUNDS)] + ["arr%d" % t for t in range(ROUNDS)])
+
+
+def rank_program(g, core, T, topo):
+    rank = T.rank_of(core)
+    if rank is None:
+        return
+    queues = {"g": g, "v": g.vector, "s": g.scalar, "t": g.tensor, "y": g.sync}
+    qsem = {"g": "qg", "v": "qv", "s": "qs", "t": "qt"}
+    total = {}
+    know = dict((q, {}) for q in queues)
+    hist = {}
+
+    def wait_for(q, sem, val, clock):
+        if know[q].get(sem, 0) >= val:
+            return
+        queues[q].wait_ge(T.sem[sem], val)
+        know[q][sem] = val
+        for s2, v2 in clock.items():
+            if know[q].get(s2, 0) < v2:
+                know[q][s2] = v2
+
+    def need(q, reads, writes, waw=True):
+        deps = []
+        for acc, isw in ((reads, False), (writes, True)):
+            for (b, lo, hi) in acc:
+                for h in hist.get(b, ()):
+                    same = h[3] == q
+                    if b.startswith("ps") and not same:
+                        deps.append(h)
+                        continue
+                    if h[1] <= lo or hi <= h[0] or not (isw or h[2]):
+                        continue
+                    if same and (q == "t" or (isw and (not h[2] or not waw))):
+                        continue
+                    deps.append(h)
+        for h in sorted(deps, key=lambda h: -h[5]):
+            wait_for(q, h[4], h[5], h[6])
+
+    def note(q, sem, val, reads, writes):
+        clock = dict(know.get(q, {}))
+        clock[sem] = max(clock.get(sem, 0), val)
+        for acc, isw in ((reads, False), (writes, True)):
+            for (b, lo, hi) in acc:
+                old = hist.get(b, [])
+                if isw and b.startswith("ps"):
+                    old = []
+                elif isw:
+                    old = [h for h in old if not (lo <= h[0] and h[1] <= hi)]
+                else:
+                    old = [h for h in old if not (h[3] == q and not h[2] and lo <= h[0] and h[1] <= hi)]
+                hist[b] = old + [(lo, hi, isw, q, sem, val, clock)]
+
+    def reg(r):
+        return r if isinstance(r, tuple) else (r, 0, int(np.prod(SCRATCH[r][1][1:])))
+
+    def do(q, call, reads, writes, waw=True):
+        R, W = [reg(r) for r in reads], [reg(w) for w in writes]
+        need(q, R, W, waw)
+        sem = qsem[q]
+        total[sem] = total.get(sem, 0) + 1
+        call(queues[q]).then_inc(T.sem[sem], 1)
+        note(q, sem, total[sem], R, W)
+
+    def dma(q, name, out, in_, reads, writes):
+        R, W = [reg(r) for r in reads], [reg(w) for w in writes]
+        need(q, R, W)
+        sem = "dma_" + name
+        total[sem] = 16
+        queues[q].dma_start(out, in_).then_inc(T.sem[sem], 16)
+        note(sem, sem, 16, R, W)
+
+    def lanes_of(src, dst):
+        return topo.engines(src, dst)[:8]
+
+    def send(dst, src, out, reads, sem):
+        need("g", [reg(r) for r in reads], [])
+        rid, pid, _ = topo.addr(dst)
+        eng = lanes_of(core, dst)
+        total["ls"] = total.get("ls", 0) + len(eng)
+        g.remote_dma(out, src, T.sem[sem], T.sem["ls"], pid, rid, sum(1 << e for e in eng))
+
+    def landed(frm, sem, name):
+        total[sem] = len(lanes_of(frm, core))
+        note("remote", sem, total[sem], [], [reg(name)])
+
+    def ts(out, in0, s1, s2, op0, op1, R, W):
+        ops = (op0,) if op1 is None else (op0, op1)
+        do("v", lambda v: v.tensor_scalar(out, in0, s1, s2, *ops), R, W)
+
+    def tt(out, a, b, op, R, W, waw=True):
+        do("v", lambda v: v.tensor_tensor(out, a, b, op), R, W, waw)
+
+    def cp(out, a, R, W):
+        do("v", lambda v: v.tensor_copy(out, a), R, W)
+
+    def ms(out, c, W):
+        do("v", lambda v: v.memset(out, c), [], W)
+
+    def scan(out, d0, d1, o0, o1, R, W):
+        do("v", lambda v: v.tensor_tensor_scan(out, d0, d1, 0.0, o0, o1), R, W)
+
+    def act(out, a, f, R, W, **kw):
+        do("s", lambda s: s.activation(out, a, f, **kw), R, W)
+
+    def mm(out, l, r, start, stop, R, W):
+        do("t", lambda x: x.matmul(out, l, r, start, stop), R, W)
+
+    def asel(out, a, pat, cmp, fill, base, mult, R, W):
+        do("g", lambda x: x.affine_select(out, a, pat, cmp, fill, base, mult), R, W)
+
+    def iota(out, pat, base, mult, W, **kw):
+        do("g", lambda x: x.iota(out, pat, base, mult, **kw), [], W)
+
+    small = {"allow_small_or_imprecise_dtypes": True}
+
+    dma("y", "in_stk", T.SI[:], T.stk[:], [], ["SI"])
+    dma("s", "in_ball", T.B[:, 0:NB], T.ball[:], [], [("B", 0, NB)])
+    dma("y", "in_wt", T.wb[:], T.wt[:], [], ["wb"])
+
+    iota(T.pI[:], [[0, 1]], 0, 1, ["pI"])
+    ms(T.of32[:], 1.0, ["of32"])
+    ms(T.ob[:], 1.0, ["ob"])
+    ms(T.c16[:], 0.0625, ["c16"])
+    ms(T.cm1[:], -1.0, ["cm1"])
+    blk = [[-16, 8], [0, 16]]
+    asel(T.LE[:], T.of32[:], blk, OP.is_equal, 0.0, 0, 1, ["of32"], ["LE"])
+    asel(T.ID[:], T.ob[:, 0:128], [[-1, 128]], OP.is_equal, 0.0, 0, 1, ["ob"], ["ID"])
+    iota(T.j16[:], [[16, 16]], 0, 0, ["j16"], **small)
+    iota(T.cm[:], [[0, 2], [1, 16]], 0, 0, ["cm"], **small)
+    asel(T.E1[:], T.ob[:, 0:144], [[-16, 9], [0, 16]], OP.is_ge, 0.0, 0, 1, ["ob"], ["E1"])
+    asel(T.E2[:], T.E1[:], [[16, 9], [0, 16]], OP.is_ge, 0.0, 15, -1, ["E1"], ["E2"])
+    asel(T.E01[:], T.E2[:], [[0, 9], [1, 16]], OP.is_equal, 0.0, -15, 0, ["E2"], ["E01"])
+    asel(T.LS[:], T.c16[:], [[-1, 128]], OP.is_equal, 0.0, -1, 1, ["c16"], ["LS"])
+    iota(T.KT[:], [[16, 16]], 0, 0, ["KT"], **small)
+    asel(T.NI[:], T.cm1[:], [[-1, 128]], OP.is_equal, 0.0, 0, 1, ["cm1"], ["NI"])
+    iota(T.rowf[:], [[16, 256]], 0, 0, ["rowf"], **small)
+    asel(T.B1[:], T.ob[:, 0:128], blk, OP.is_ge, 0.0, 0, 1, ["ob"], ["B1"])
+    asel(T.BO[:], T.B1[:], [[16, 8], [0, 16]], OP.is_ge, 0.0, 15, -1, ["B1"], ["BO"])
+
+    ms(T.WN[:], 1.0, ["WN"])
+    ms(T.RS[:], 1.0, ["RS"])
+    ms(T.RS[:, 1:CW:16], 0.0, ["RS"])
+    ms(T.KS[:], -1.0, ["KS"])
+    ms(T.KS[:, 0:256:16], 100.0, ["KS"])
+    ms(T.B[:, NB:NB + DUMP], 0.0, [("B", NB, NB + DUMP)])
+    ms(T.D[:, 256:272], 0.0, [("D", 256, 272)])
+    ms(T.vraw[:, 256:272], 0.0, [("vraw", 256, 272)])
+    cp(T.SU[:], T.SI[:], ["SI"], ["SU"])
+
+    def factors():
+        ts(T.eI[:], T.SI[:], 1023, None, OP.bitwise_and, None, ["SI"], ["eI"])
+        ts(T.S16[:], T.SI[:], 16.0, None, OP.mult, None, ["SI"], ["S16"])
+        ts(T.ef[:], T.eI[:], 2.0, 1.0, OP.mult, OP.add, ["eI"], ["ef"])
+        mm(T.psE[:, 0:256], T.LE[:], T.ef[:], True, True, ["LE", "ef"], ["psE"])
+
+    def early_constants():
+        ts(T.rI[:], T.pI[:], 15, None, OP.bitwise_and, None, ["pI"], ["rI"])
+        cp(T.rc[:], T.rI[:], ["rI"], ["rc"])
+        ts(T.iF[:], T.j16[:], T.rc[:], None, OP.add, None, ["j16", "rc"], ["iF"])
+        ts(T.d16[:], T.rc[:], 16.0, None, OP.mult, None, ["rc"], ["d16"])
+        ts(T.nc[:, 0:1], T.rc[:], 0.0, None, OP.add, None, ["rc"], [("nc", 0, 1)])
+        ts(T.nc[:, 1:2], T.rc[:], 16.0, None, OP.add, None, ["rc"], [("nc", 1, 2)])
+        ts(T.KB[:], T.iF[:], 16.0, 14.0, OP.mult, OP.add, ["iF"], ["KB"])
+        ts(T.iL[:], T.iF[:], 16.0, None, OP.mult, None, ["iF"], ["iL"])
+        ts(T.DM[:], T.cm[:], T.rc[:], None, OP.is_equal, None, ["cm", "rc"], ["DM"])
+        ts(T.bs[:], T.nc[:], -1.0, -0.5, OP.mult, OP.add, ["nc"], ["bs"])
+        ts(T.dm[:], T.nc[:], float(NB), None, OP.add, None, ["nc"], ["dm"])
+        cp(T.wI[:], T.wb[:], ["wb"], ["wI"])
+        ts(T.wA[:], T.wI[:], 15, None, OP.bitwise_and, None, ["wI"], ["wA"])
+        ts(T.wf[:], T.wA[:], 4096.0, None, OP.mult, None, ["wA"], ["wf"])
+
+    def late_constants():
+        cp(T.row[:], T.rowf[:], ["rowf"], ["row"])
+        ts(T.WE[:], T.E01[:], T.wf[:], None, OP.mult, None, ["E01", "wf"], ["WE"])
+        ts(T.WB[:], T.BO[:], T.wf[:], None, OP.mult, None, ["BO", "wf"], ["WB"])
+
+    for t in range(ROUNDS):
+        last = t == ROUNDS - 1
+        factors()
+        if t == 0:
+            early_constants()
+        n = len(T.cores)
+        dst, frm = T.cores[(rank + t + 1) % n], T.cores[(rank - t - 1) % n]
+        CHn, PKn, RXn, RCn = "CH%d" % t, "PK%d" % t, "RX%d" % t, "RC%d" % t
+
+        def part(name, c):
+            return (name, CW * c, CW * c + CW)
+
+        def xcopy(c):
+            b = "psX%d" % (c % 2)
+            mm(T[b][:, 0:64], T.ID[:], T.P[:, CW * c:CW * c + CW:16], True, True, ["ID", part("P", c)], [b])
+
+        def votes(c):
+            for q in range(16):
+                mm(T.psV[:, 64 * c:64 * c + 64], T.E01[:, 15 - q:143 - q], T.WN[:, 4 * c:4 * c + 4, 16 * q:16 * q + 16],
+                   q == 0, q == 15, ["E01", part("WN", c)], ["psV"])
+
+        for c in range(CH):
+            act(T.P[:, CW * c:CW * c + CW], T.B[:, 0:NB].indirect(T.SU[:, 64 * c:64 * c + 64]), AF.Copy,
+                [("B", 0, NB), "SU"], [part("P", c)])
+        xcopy(0)
+        xcopy(1)
+        for c in range(CH):
+            b = "psX%d" % (c % 2)
+            for d in range(1, 16):
+                tt(T.WN[:, 4 * c:4 * c + 4, d:256:16], T.P[:, CW * c + d:CW * c + CW:16], T[b][:, 0:64], OP.is_lt,
+                   [part("P", c), b], [part("WN", c)], waw=False)
+            if c + 2 < CH:
+                xcopy(c + 2)
+            votes(c)
+            if c == 0:
+                tt(T.zu[:], T.S16[:], T.psE[:, 0:256], OP.mult, ["S16", "psE"], ["zu"])
+                mm(T.psD[:, 0:256], T.LS[:], T.zu[:], True, False, ["LS", "zu"], ["psD"])
+            if t == 0 and c == 1:
+                late_constants()
+            scan(T.PM[:, CW * c:CW * c + CW], T.RS[:], T.P[:, CW * c:CW * c + CW], OP.mult, OP.max,
+                 ["RS", part("P", c)], [part("PM", c)])
+        ms(T.PM[:, 0:NB:16], 255.0, ["PM"])
+        mm(T.psD[:, 0:256], T.NI[:], T.S16[:], False, True, ["NI", "S16"], ["psD"])
+
+        ts(T.tw[:], T.psV[:, 0:256], 9.0, 16.0, OP.is_ge, OP.mult, ["psV"], ["tw"])
+        scan(T.st[:], T.KS[:], T.tw[:], OP.add, OP.min, ["KS", "tw"], ["st"])
+        tt(T.kb[:], T.st[:, 15:256:16], T.KB[:], OP.add, ["st", "KB"], ["kb"])
+        ts(T.kl0[:], T.st[:, 15:256:16], 14.0, None, OP.add, None, ["st"], ["kl0"])
+        cp(T.kl1[:], T.kb[:], ["kb"], ["kl1"])
+        act(T.K[:], T.KT[:, 0:16].indirect(T.kl0[:, 0:16]), AF.Copy, ["KT", "kl0"], ["K", "A16"], accum_out=T.A16[:])
+        tt(T.D[:, 0:256], T.PM[:, 0:NB].indirect(T.kl1[:, 0:16]), T.P[:, 0:NB:16], OP.subtract, ["PM", "kl1", "P"], [("D", 0, 256)])
+        act(T.Y[:], T.D[:, 0:256], AF.Abs, [("D", 0, 256)], ["Y"])
+        mm(T.psL[:, 0:16], T.ID[:], T.iL[:], True, False, ["ID", "iL"], ["psL"])
+        for q in range(16):
+            mm(T.psL[:, 0:16], T.WE[:, 15 - q:143 - q], T.Y[:, q:256:16], False, q == 15, ["WE", "Y"], ["psL"])
+        for b in ("psR", "psS"):
+            mm(T[b][:, 0:256], T.ob[0:1, 0:128], T.row[0:1, :], True, False, ["ob", "row"], [b])
+            if b == "psS":
+                mm(T[b][:, 0:256], T.NI[:], T.S16[:], False, False, ["NI", "S16"], [b])
+            mm(T[b][:, 0:256], T.WB[:], T.Y[:], False, True, ["WB", "Y"], [b])
+
+        ts(T.HF[:], T.K[:], 160.0, None, OP.is_ge, None, ["K"], ["HF"])
+        scan(T[CHn][:], T.ob[:], T.HF[:], OP.mult, OP.add, ["ob", "HF"], [CHn])
+        send(dst, T[CHn][:, 255:256], T[RCn][:], [CHn], "cnt%d" % t)
+        for c in range(2):
+            act(T.J[:], T[CHn][:], AF.Sign, [CHn, "bs"], ["J", ("acch", c, c + 1)], bias=T.bs[:, c:c + 1], accum_out=T.acch[:, c:c + 1])
+        ts(T.ZF[:], T.K[:], 8.0, None, OP.is_lt, None, ["K"], ["ZF"])
+        ts(T.A4[:], T.A16[:], 256.0, None, OP.mult, None, ["A16"], ["A4"])
+        scan(T.CZ[:], T.ob[:], T.ZF[:], OP.mult, OP.add, ["ob", "ZF"], ["CZ"])
+        ts(T.C[:], T.K[:], T.d16[:], None, OP.is_gt, None, ["K", "d16"], ["C"])
+        ts(T.EK[:], T.K[:], T.d16[:], None, OP.is_equal, None, ["K", "d16"], ["EK"])
+        ts(T.hl[:], T.acch[:], -0.5, 128.0, OP.mult, OP.add, ["acch"], ["hl"])
+        act(T[PKn][:], T.D[:, 0:272].indirect(T.hl[:, 0:2]), AF.Abs, ["D", "hl"], [PKn])
+        send(dst, T[PKn][:], T[RXn][:], [PKn], "arr%d" % t)
+        landed(frm, "cnt%d" % t, RCn)
+        landed(frm, "arr%d" % t, RXn)
+
+        act(T.psD[:, 0:256], T.psD[:, 0:256], AF.Identity, ["psD", "A16"], ["psD"], bias=T.A16[:])
+        for c in range(2):
+            act(T.J[:], T.CZ[:], AF.Sign, ["CZ", "bs"], ["J", ("accz", c, c + 1)], bias=T.bs[:, c:c + 1], accum_out=T.accz[:, c:c + 1])
+        act(T.vraw[:, 0:256], T.psR[:, 0:256], AF.Identity, ["psR", "A4"], [("vraw", 0, 256)], bias=T.A4[:])
+        act(T.psS[:, 0:256], T.psS[:, 0:256], AF.Identity, ["psS", "A4"], ["psS"], bias=T.A4[:])
+
+        ts(T.VI[:], T.psL[:, 0:16], T.A4[:], None, OP.add, None, ["psL", "A4"], ["VI"])
+        ts(T.VB[:], T.VI[:], 4, 4095, OP.arith_shift_right, OP.bitwise_and, ["VI"], ["VB"])
+        cp(T.VL[:], T.VB[:], ["VB"], ["VL"])
+        cp(T.B[:, 0:NB + DUMP].indirect(T.VL[:, 0:16]), T.Y[:], ["VL", "Y"], ["B"])
+        ts(T.zl[:], T.accz[:], -0.5, 128.0, OP.mult, OP.add, ["accz"], ["zl"])
+        act(T.G32[:], T.vraw[:, 0:272].indirect(T.zl[:, 0:2]), AF.Copy, ["vraw", "zl"], ["G32"])
+
+        def stacks():
+            tt(T.psD[:, 0:256], T.psD[:, 0:256], T.C[:], OP.mult, ["psD", "C"], ["psD"])
+            tt(T.t3[:], T.psS[:, 0:256], T.EK[:], OP.mult, ["psS", "EK"], ["t3"])
+            tt(T.psD[:, 0:256], T.psD[:, 0:256], T.S16[:], OP.add, ["psD", "S16"], ["psD"])
+            tt(T.UI[:], T.psD[:, 0:256], T.t3[:], OP.add, ["psD", "t3"], ["UI"])
+            ts(T.SI[:], T.UI[:], 4, 4095, OP.arith_shift_right, OP.bitwise_and, ["UI"], ["SI"])
+            if last:
+                cp(T.yof[:], T.SI[:], ["SI"], ["yof"])
+            else:
+                cp(T.SU[:], T.SI[:], ["SI"], ["SU"])
+
+        def arrivals():
+            tt(T.GM[:], T.G32[:], T.DM[:], OP.mult, ["G32", "DM"], ["GM"])
+            tt(T.mn[:], T[RCn][:], T.CZ[:, 255:256], OP.min, [RCn, "CZ"], ["mn"])
+            for c in range(2):
+                do("v", lambda v: v.tensor_reduce(T.rd[:, c:c + 1], T.GM[:, 16 * c:16 * c + 16], AxisListType.X, OP.add),
+                   ["GM"], [("rd", c, c + 1)])
+            ts(T.nk[:], T.nc[:], T.mn[:], None, OP.is_ge, None, ["nc", "mn"], ["nk"])
+            cp(T.ri[:], T.rd[:], ["rd"], ["ri"])
+            tt(T.nd[:], T.nk[:], T.dm[:], OP.mult, ["nk", "dm"], ["nd"])
+            ts(T.rb[:], T.ri[:], 4, 4095, OP.arith_shift_right, OP.bitwise_and, ["ri"], ["rb"])
+            tt(T.of[:], T.rb[:], T.nd[:], OP.max, ["rb", "nd"], ["of"])
+            cp(T.OL[:], T.of[:], ["of"], ["OL"])
+            cp(T.B[:, 0:NB + DUMP].indirect(T.OL[:, 0:2]), T[RXn][:], ["OL", RXn], ["B"])
+
+        if last:
+            arrivals()
+            dma("y", "out_yb", T.yb[:], T.B[:, 0:NB], [("B", 0, NB)], [])
+            stacks()
+            dma("s", "out_yo", T.yo[:], T.yof[:], ["yof"], [])
+        else:
+            stacks()
+            arrivals()
+
+    for sem in sorted(total):
+        wait_for("g", sem, total[sem], {})

@@ -8,6 +8,7 @@ NB = 4096
 DUMP = 32
 CH = 4
 CW = NB // CH
+REP = 4
 
 SCRATCH = {}
 
@@ -17,20 +18,19 @@ def _declare(where, dtype, **shapes):
         SCRATCH[name] = (where, [128] + (n if isinstance(n, list) else [n]), dtype)
 
 
-_declare("sbuf", "bfloat16", B=NB + DUMP, P=NB, PM=NB, WN=[16, 256], tw=256, st=256, K=256, D=272, Y=256, HF=256, ZF=256,
-         CZ=256, J=256, C=256, EK=256, ob=256, ID=128, B1=128, BO=128, WB=128, E1=144, E2=144, E01=144, WE=144, RS=CW,
-         KS=256, KT=16, iL=16, row=256, wb=1,
-         CH0=256, CH1=256, CH2=256, PK0=32, PK1=32, PK2=32, RX0=32, RX1=32, RX2=32, RC0=1, RC1=1, RC2=1)
-_declare("sbuf", "float32", S16=256, kb=16, A16=1, A4=1, acch=2, accz=2, vraw=272, G32=32, GM=32, rd=2, mn=1, nk=2, nd=2,
-         of=2, ef=256, zu=256, t3=256, yof=256, of32=128, c16=128, cm1=128, LE=128, LS=128, NI=128, rc=1, d16=1, bs=2,
+_declare("sbuf", "bfloat16", B=NB + DUMP, P=NB, PM=NB, pat=64, WN=[16, 256], tw=256, st=256, K=256, D=256, Y=272, HF=256,
+         ZF=256, CH=256, CZ=256, J0=256, J1=256, C=256, EK=256, ob=256, o256=256, r57=256, ID=128, B1=128, BO=128, BA=128,
+         WB=128, E1=144, E2=144, E01=144, WE=144, RS=CW, KS=256, KT=16, HT=16, ET=16, iL=16, row=256, wb=1, OW=32, u=32,
+         w=32, PK0=32, PK1=32, PK2=32, RX0=32, RX1=32, RX2=32)
+_declare("sbuf", "float32", S16=256, kb=16, krr=1, acca=2, accb=2, accp=2, accz=2, vraw=272, G32=32, GM=32, rd=2, nk=2,
+         nd=2, ef=256, zu=256, t3=256, yof=256, of32=128, c16=128, cm1=128, LE=128, LS=128, NI=128, rc=1, d16=1, bs=2,
          nc=2, dm=2, j16=16, iF=16, KB=16, rowf=256, cm=32, DM=32, wf=1)
 _declare("sbuf", "int32", SI=256, eI=256, UI=256, VI=16, VB=16, ri=2, rb=2, pI=1, rI=1, wI=1, wA=1)
 _declare("sbuf", "uint16", SU=256, kl0=16, kl1=16, hl=2, zl=2, OL=2, VL=16)
 _declare("psum", "float32", psX0=512, psX1=512, psV=512, psE=512, psD=512, psS=512, psR=512, psL=512)
 
 DMAS = ["in_stk", "in_wt", "in_ball", "out_yo", "out_yb"]
-SEMAPHORES = (["qv", "qs", "qt", "qg", "ls"] + ["dma_" + d for d in DMAS]
-              + ["cnt%d" % t for t in range(ROUNDS)] + ["arr%d" % t for t in range(ROUNDS)])
+SEMAPHORES = ["qv", "qs", "qt", "qg", "ls"] + ["dma_" + d for d in DMAS] + ["arr%d" % t for t in range(ROUNDS)]
 
 
 def rank_program(g, core, T, topo):
@@ -129,8 +129,8 @@ def rank_program(g, core, T, topo):
     def ms(out, c, W):
         do("v", lambda v: v.memset(out, c), [], W)
 
-    def scan(out, d0, d1, o0, o1, R, W):
-        do("v", lambda v: v.tensor_tensor_scan(out, d0, d1, 0.0, o0, o1), R, W)
+    def scan(out, d0, d1, o0, o1, R, W, ini=0.0):
+        do("v", lambda v: v.tensor_tensor_scan(out, d0, d1, ini, o0, o1), R, W)
 
     def act(out, a, f, R, W, **kw):
         do("s", lambda s: s.activation(out, a, f, **kw), R, W)
@@ -152,48 +152,48 @@ def rank_program(g, core, T, topo):
 
     iota(T.pI[:], [[0, 1]], 0, 1, ["pI"])
     ms(T.of32[:], 1.0, ["of32"])
+    ms(T.cm1[:], -1.0, ["cm1"])
     ms(T.ob[:], 1.0, ["ob"])
     ms(T.c16[:], 0.0625, ["c16"])
-    ms(T.cm1[:], -1.0, ["cm1"])
     blk = [[-16, 8], [0, 16]]
     asel(T.LE[:], T.of32[:], blk, OP.is_equal, 0.0, 0, 1, ["of32"], ["LE"])
     asel(T.ID[:], T.ob[:, 0:128], [[-1, 128]], OP.is_equal, 0.0, 0, 1, ["ob"], ["ID"])
+    asel(T.NI[:], T.cm1[:], [[-1, 128]], OP.is_equal, 0.0, 0, 1, ["cm1"], ["NI"])
+    iota(T.rowf[:], [[16, 256]], 0, 0, ["rowf"], **small)
     iota(T.j16[:], [[16, 16]], 0, 0, ["j16"], **small)
     iota(T.cm[:], [[0, 2], [1, 16]], 0, 0, ["cm"], **small)
+    iota(T.KT[:], [[16, 16]], 0, 0, ["KT"], **small)
     asel(T.E1[:], T.ob[:, 0:144], [[-16, 9], [0, 16]], OP.is_ge, 0.0, 0, 1, ["ob"], ["E1"])
     asel(T.E2[:], T.E1[:], [[16, 9], [0, 16]], OP.is_ge, 0.0, 15, -1, ["E1"], ["E2"])
     asel(T.E01[:], T.E2[:], [[0, 9], [1, 16]], OP.is_equal, 0.0, -15, 0, ["E2"], ["E01"])
     asel(T.LS[:], T.c16[:], [[-1, 128]], OP.is_equal, 0.0, -1, 1, ["c16"], ["LS"])
-    iota(T.KT[:], [[16, 16]], 0, 0, ["KT"], **small)
-    asel(T.NI[:], T.cm1[:], [[-1, 128]], OP.is_equal, 0.0, 0, 1, ["cm1"], ["NI"])
-    iota(T.rowf[:], [[16, 256]], 0, 0, ["rowf"], **small)
     asel(T.B1[:], T.ob[:, 0:128], blk, OP.is_ge, 0.0, 0, 1, ["ob"], ["B1"])
     asel(T.BO[:], T.B1[:], [[16, 8], [0, 16]], OP.is_ge, 0.0, 15, -1, ["B1"], ["BO"])
 
-    ms(T.WN[:], 1.0, ["WN"])
+    ms(T.pat[:], 0.0, ["pat"])
     ms(T.RS[:], 1.0, ["RS"])
+    ms(T.r57[:], 57344.0, ["r57"])
     ms(T.RS[:, 1:CW:16], 0.0, ["RS"])
     ms(T.KS[:], -1.0, ["KS"])
+    ms(T.pat[:, 0:64:16], 16.0, ["pat"])
+    ms(T.o256[:], 256.0, ["o256"])
     ms(T.KS[:, 0:256:16], 100.0, ["KS"])
     ms(T.B[:, NB:NB + DUMP], 0.0, [("B", NB, NB + DUMP)])
-    ms(T.D[:, 256:272], 0.0, [("D", 256, 272)])
+    ms(T.Y[:, 256:272], -512.0, [("Y", 256, 272)])
     ms(T.vraw[:, 256:272], 0.0, [("vraw", 256, 272)])
     cp(T.SU[:], T.SI[:], ["SI"], ["SU"])
 
-    def factors():
-        ts(T.eI[:], T.SI[:], 1023, None, OP.bitwise_and, None, ["SI"], ["eI"])
-        ts(T.S16[:], T.SI[:], 16.0, None, OP.mult, None, ["SI"], ["S16"])
-        ts(T.ef[:], T.eI[:], 2.0, 1.0, OP.mult, OP.add, ["eI"], ["ef"])
-        mm(T.psE[:, 0:256], T.LE[:], T.ef[:], True, True, ["LE", "ef"], ["psE"])
-
     def early_constants():
         ts(T.rI[:], T.pI[:], 15, None, OP.bitwise_and, None, ["pI"], ["rI"])
+        cp(T.row[:], T.rowf[:], ["rowf"], ["row"])
         cp(T.rc[:], T.rI[:], ["rI"], ["rc"])
+        ts(T.HT[:], T.KT[:], 160.0, None, OP.is_ge, None, ["KT"], ["HT"])
         ts(T.iF[:], T.j16[:], T.rc[:], None, OP.add, None, ["j16", "rc"], ["iF"])
         ts(T.d16[:], T.rc[:], 16.0, None, OP.mult, None, ["rc"], ["d16"])
         ts(T.nc[:, 0:1], T.rc[:], 0.0, None, OP.add, None, ["rc"], [("nc", 0, 1)])
         ts(T.nc[:, 1:2], T.rc[:], 16.0, None, OP.add, None, ["rc"], [("nc", 1, 2)])
         ts(T.KB[:], T.iF[:], 16.0, 14.0, OP.mult, OP.add, ["iF"], ["KB"])
+        ts(T.ET[:], T.KT[:], T.d16[:], None, OP.is_equal, None, ["KT", "d16"], ["ET"])
         ts(T.iL[:], T.iF[:], 16.0, None, OP.mult, None, ["iF"], ["iL"])
         ts(T.DM[:], T.cm[:], T.rc[:], None, OP.is_equal, None, ["cm", "rc"], ["DM"])
         ts(T.bs[:], T.nc[:], -1.0, -0.5, OP.mult, OP.add, ["nc"], ["bs"])
@@ -203,133 +203,192 @@ def rank_program(g, core, T, topo):
         ts(T.wf[:], T.wA[:], 4096.0, None, OP.mult, None, ["wA"], ["wf"])
 
     def late_constants():
-        cp(T.row[:], T.rowf[:], ["rowf"], ["row"])
         ts(T.WE[:], T.E01[:], T.wf[:], None, OP.mult, None, ["E01", "wf"], ["WE"])
         ts(T.WB[:], T.BO[:], T.wf[:], None, OP.mult, None, ["BO", "wf"], ["WB"])
 
+    balls, spare = T.B[:, 0:NB], T.B[:, 0:NB + DUMP]
+    ones, row = T.ob[0:1, 0:128], T.row[0:1, :]
+    psD, psS, psR, psL = T.psD[:, 0:256], T.psS[:, 0:256], T.psR[:, 0:256], T.psL[:, 0:16]
+
+    def factors():
+        ts(T.eI[:], T.SI[:], 1023, None, OP.bitwise_and, None, ["SI"], ["eI"])
+        ts(T.S16[:], T.SI[:], 16.0, None, OP.mult, None, ["SI"], ["S16"])
+        ts(T.ef[:], T.eI[:], 2.0, 1.0, OP.mult, OP.add, ["eI"], ["ef"])
+        mm(T.psE[:, 0:256], T.LE[:], T.ef[:], True, True, ["LE", "ef"], ["psE"])
+
+    factors()
+    early_constants()
+
     for t in range(ROUNDS):
         last = t == ROUNDS - 1
-        factors()
-        if t == 0:
-            early_constants()
         n = len(T.cores)
         dst, frm = T.cores[(rank + t + 1) % n], T.cores[(rank - t - 1) % n]
-        CHn, PKn, RXn, RCn = "CH%d" % t, "PK%d" % t, "RX%d" % t, "RC%d" % t
+        PKn, RXn = "PK%d" % t, "RX%d" % t
 
         def part(name, c):
             return (name, CW * c, CW * c + CW)
 
-        def xcopy(c):
-            b = "psX%d" % (c % 2)
-            mm(T[b][:, 0:64], T.ID[:], T.P[:, CW * c:CW * c + CW:16], True, True, ["ID", part("P", c)], [b])
+        def gather(q, a, b):
+            out, off = T.P[:, 16 * a:16 * b], T.SU[:, a:b]
+            R, W = [("B", 0, NB), ("SU", a, b)], [("P", 16 * a, 16 * b)]
+            if q == "s":
+                act(out, balls.indirect(off), AF.Copy, R, W)
+            else:
+                cp(out, balls.indirect(off), R, W)
 
-        def votes(c):
+        def tops(c):
+            b = "psX%d" % (c % 2)
+            for r in range(REP):
+                mm(T[b][:, r:64 * REP:REP], T.ID[:], T.P[:, CW * c:CW * c + CW:16], True, True, ["ID", part("P", c)], [b])
+
+        def compare(c):
+            b, s = "psX%d" % (c % 2), 16 // REP
+            for d in range(s):
+                tt(T.WN[:, 4 * c:4 * c + 4, d:256:s], T.P[:, CW * c + d:CW * c + CW:s], T[b][:, 0:64 * REP],
+                   OP.is_lt, [part("P", c), b], [part("WN", c)], waw=False)
+
+        def votes(c, b):
+            mm(T[b][:, 64 * c:64 * c + 64], ones, T.pat[0:1, :], True, False, ["ob", "pat"], [b])
             for q in range(16):
-                mm(T.psV[:, 64 * c:64 * c + 64], T.E01[:, 15 - q:143 - q], T.WN[:, 4 * c:4 * c + 4, 16 * q:16 * q + 16],
-                   q == 0, q == 15, ["E01", part("WN", c)], ["psV"])
+                mm(T[b][:, 64 * c:64 * c + 64], T.E01[:, 15 - q:143 - q], T.WN[:, 4 * c:4 * c + 4, 16 * q:16 * q + 16],
+                   False, q == 15, ["E01", part("WN", c)], [b])
 
-        for c in range(CH):
-            act(T.P[:, CW * c:CW * c + CW], T.B[:, 0:NB].indirect(T.SU[:, 64 * c:64 * c + 64]), AF.Copy,
-                [("B", 0, NB), "SU"], [part("P", c)])
-        xcopy(0)
-        xcopy(1)
-        for c in range(CH):
-            b = "psX%d" % (c % 2)
-            for d in range(1, 16):
-                tt(T.WN[:, 4 * c:4 * c + 4, d:256:16], T.P[:, CW * c + d:CW * c + CW:16], T[b][:, 0:64], OP.is_lt,
-                   [part("P", c), b], [part("WN", c)], waw=False)
-            if c + 2 < CH:
-                xcopy(c + 2)
-            votes(c)
-            if c == 0:
-                tt(T.zu[:], T.S16[:], T.psE[:, 0:256], OP.mult, ["S16", "psE"], ["zu"])
-                mm(T.psD[:, 0:256], T.LS[:], T.zu[:], True, False, ["LS", "zu"], ["psD"])
-            if t == 0 and c == 1:
-                late_constants()
+        def prefix(c):
             scan(T.PM[:, CW * c:CW * c + CW], T.RS[:], T.P[:, CW * c:CW * c + CW], OP.mult, OP.max,
                  ["RS", part("P", c)], [part("PM", c)])
-        ms(T.PM[:, 0:NB:16], 255.0, ["PM"])
-        mm(T.psD[:, 0:256], T.NI[:], T.S16[:], False, True, ["NI", "S16"], ["psD"])
 
-        ts(T.tw[:], T.psV[:, 0:256], 9.0, 16.0, OP.is_ge, OP.mult, ["psV"], ["tw"])
-        scan(T.st[:], T.KS[:], T.tw[:], OP.add, OP.min, ["KS", "tw"], ["st"])
-        tt(T.kb[:], T.st[:, 15:256:16], T.KB[:], OP.add, ["st", "KB"], ["kb"])
-        ts(T.kl0[:], T.st[:, 15:256:16], 14.0, None, OP.add, None, ["st"], ["kl0"])
-        cp(T.kl1[:], T.kb[:], ["kb"], ["kl1"])
-        act(T.K[:], T.KT[:, 0:16].indirect(T.kl0[:, 0:16]), AF.Copy, ["KT", "kl0"], ["K", "A16"], accum_out=T.A16[:])
-        tt(T.D[:, 0:256], T.PM[:, 0:NB].indirect(T.kl1[:, 0:16]), T.P[:, 0:NB:16], OP.subtract, ["PM", "kl1", "P"], [("D", 0, 256)])
-        act(T.Y[:], T.D[:, 0:256], AF.Abs, [("D", 0, 256)], ["Y"])
-        mm(T.psL[:, 0:16], T.ID[:], T.iL[:], True, False, ["ID", "iL"], ["psL"])
-        for q in range(16):
-            mm(T.psL[:, 0:16], T.WE[:, 15 - q:143 - q], T.Y[:, q:256:16], False, q == 15, ["WE", "Y"], ["psL"])
-        for b in ("psR", "psS"):
-            mm(T[b][:, 0:256], T.ob[0:1, 0:128], T.row[0:1, :], True, False, ["ob", "row"], [b])
-            if b == "psS":
-                mm(T[b][:, 0:256], T.NI[:], T.S16[:], False, False, ["NI", "S16"], [b])
-            mm(T[b][:, 0:256], T.WB[:], T.Y[:], False, True, ["WB", "Y"], [b])
+        def filled(c, e):
+            a, e = CW * c, CW * e
+            act(T.PM[:, a:e:16], T.P[:, a:e:16], AF.Identity, [("P", a, e)], [("PM", a, e)], bias=255.0, scale=0.0)
 
-        ts(T.HF[:], T.K[:], 160.0, None, OP.is_ge, None, ["K"], ["HF"])
-        scan(T[CHn][:], T.ob[:], T.HF[:], OP.mult, OP.add, ["ob", "HF"], [CHn])
-        send(dst, T[CHn][:, 255:256], T[RCn][:], [CHn], "cnt%d" % t)
-        for c in range(2):
-            act(T.J[:], T[CHn][:], AF.Sign, [CHn, "bs"], ["J", ("acch", c, c + 1)], bias=T.bs[:, c:c + 1], accum_out=T.acch[:, c:c + 1])
-        ts(T.ZF[:], T.K[:], 8.0, None, OP.is_lt, None, ["K"], ["ZF"])
-        ts(T.A4[:], T.A16[:], 256.0, None, OP.mult, None, ["A16"], ["A4"])
-        scan(T.CZ[:], T.ob[:], T.ZF[:], OP.mult, OP.add, ["ob", "ZF"], ["CZ"])
-        ts(T.C[:], T.K[:], T.d16[:], None, OP.is_gt, None, ["K", "d16"], ["C"])
-        ts(T.EK[:], T.K[:], T.d16[:], None, OP.is_equal, None, ["K", "d16"], ["EK"])
-        ts(T.hl[:], T.acch[:], -0.5, 128.0, OP.mult, OP.add, ["acch"], ["hl"])
-        act(T[PKn][:], T.D[:, 0:272].indirect(T.hl[:, 0:2]), AF.Abs, ["D", "hl"], [PKn])
-        send(dst, T[PKn][:], T[RXn][:], [PKn], "arr%d" % t)
-        landed(frm, "cnt%d" % t, RCn)
-        landed(frm, "arr%d" % t, RXn)
+        def won(a, e, b):
+            ts(T.tw[:, a:e], T[b][:, a:e], 9.0, 16.0, OP.is_ge, OP.mult, [b], [("tw", a, e)])
 
-        act(T.psD[:, 0:256], T.psD[:, 0:256], AF.Identity, ["psD", "A16"], ["psD"], bias=T.A16[:])
-        for c in range(2):
-            act(T.J[:], T.CZ[:], AF.Sign, ["CZ", "bs"], ["J", ("accz", c, c + 1)], bias=T.bs[:, c:c + 1], accum_out=T.accz[:, c:c + 1])
-        act(T.vraw[:, 0:256], T.psR[:, 0:256], AF.Identity, ["psR", "A4"], [("vraw", 0, 256)], bias=T.A4[:])
-        act(T.psS[:, 0:256], T.psS[:, 0:256], AF.Identity, ["psS", "A4"], ["psS"], bias=T.A4[:])
+        def runs(a, e):
+            scan(T.st[:, a:e], T.KS[:, a:e], T.tw[:, a:e], OP.add, OP.min, ["KS", ("tw", a, e)], [("st", a, e)])
 
-        ts(T.VI[:], T.psL[:, 0:16], T.A4[:], None, OP.add, None, ["psL", "A4"], ["VI"])
-        ts(T.VB[:], T.VI[:], 4, 4095, OP.arith_shift_right, OP.bitwise_and, ["VI"], ["VB"])
-        cp(T.VL[:], T.VB[:], ["VB"], ["VL"])
-        cp(T.B[:, 0:NB + DUMP].indirect(T.VL[:, 0:16]), T.Y[:], ["VL", "Y"], ["B"])
-        ts(T.zl[:], T.accz[:], -0.5, 128.0, OP.mult, OP.add, ["accz"], ["zl"])
-        act(T.G32[:], T.vraw[:, 0:272].indirect(T.zl[:, 0:2]), AF.Copy, ["vraw", "zl"], ["G32"])
+        def klist(j, e):
+            ts(T.kl0[:, j:e], T.st[:, 16 * j + 15:16 * e:16], 14.0, None, OP.add, None, [("st", 16 * j, 16 * e)], [("kl0", j, e)])
 
-        def stacks():
-            tt(T.psD[:, 0:256], T.psD[:, 0:256], T.C[:], OP.mult, ["psD", "C"], ["psD"])
-            tt(T.t3[:], T.psS[:, 0:256], T.EK[:], OP.mult, ["psS", "EK"], ["t3"])
-            tt(T.psD[:, 0:256], T.psD[:, 0:256], T.S16[:], OP.add, ["psD", "S16"], ["psD"])
-            tt(T.UI[:], T.psD[:, 0:256], T.t3[:], OP.add, ["psD", "t3"], ["UI"])
-            ts(T.SI[:], T.UI[:], 4, 4095, OP.arith_shift_right, OP.bitwise_and, ["UI"], ["SI"])
-            if last:
-                cp(T.yof[:], T.SI[:], ["SI"], ["yof"])
-            else:
-                cp(T.SU[:], T.SI[:], ["SI"], ["SU"])
+        def high(j, e):
+            act(T.HF[:, 16 * j:16 * e], T.HT[:, 0:16].indirect(T.kl0[:, j:e]), AF.Copy, ["HT", ("kl0", j, e)], [("HF", 16 * j, 16 * e)])
 
-        def arrivals():
-            tt(T.GM[:], T.G32[:], T.DM[:], OP.mult, ["G32", "DM"], ["GM"])
-            tt(T.mn[:], T[RCn][:], T.CZ[:, 255:256], OP.min, [RCn, "CZ"], ["mn"])
+        def count(a, e, acc):
             for c in range(2):
-                do("v", lambda v: v.tensor_reduce(T.rd[:, c:c + 1], T.GM[:, 16 * c:16 * c + 16], AxisListType.X, OP.add),
-                   ["GM"], [("rd", c, c + 1)])
-            ts(T.nk[:], T.nc[:], T.mn[:], None, OP.is_ge, None, ["nc", "mn"], ["nk"])
-            cp(T.ri[:], T.rd[:], ["rd"], ["ri"])
-            tt(T.nd[:], T.nk[:], T.dm[:], OP.mult, ["nk", "dm"], ["nd"])
-            ts(T.rb[:], T.ri[:], 4, 4095, OP.arith_shift_right, OP.bitwise_and, ["ri"], ["rb"])
-            tt(T.of[:], T.rb[:], T.nd[:], OP.max, ["rb", "nd"], ["of"])
-            cp(T.OL[:], T.of[:], ["of"], ["OL"])
-            cp(T.B[:, 0:NB + DUMP].indirect(T.OL[:, 0:2]), T[RXn][:], ["OL", RXn], ["B"])
+                act(T["J%d" % c][:, a:e], T.CH[:, a:e], AF.Sign, [("CH", a, e), "bs"], ["J%d" % c, (acc, c, c + 1)],
+                    bias=T.bs[:, c:c + 1], accum_out=T[acc][:, c:c + 1])
 
+        gather("s", 0, 32)
+        gather("v", 32, 64)
+        gather("s", 64, 128)
+        gather("s", 128, 192)
+        gather("s", 192, 256)
+        tops(0)
+        compare(0)
+        mm(psD, T.NI[:], T.S16[:], True, False, ["NI", "S16"], ["psD"])
+        mm(psD, ones, T.r57[0:1, :], False, False, ["ob", "r57"], ["psD"])
+        mm(psR, ones, row, True, False, ["ob", "row"], ["psR"])
+        mm(psL, T.ID[:], T.iL[:], True, False, ["ID", "iL"], ["psL"])
+        tops(1)
+        votes(0, "psV")
+        tt(T.zu[:], T.S16[:], T.psE[:, 0:256], OP.mult, ["S16", "psE"], ["zu"])
+        tops(2)
+        prefix(0)
+        compare(1)
+        votes(1, "psV")
+        mm(psD, T.LS[:], T.zu[:], False, False, ["LS", "zu"], ["psD"])
+        if t == 0:
+            late_constants()
+        tops(3)
+        prefix(1)
+        compare(2)
+        votes(2, "psV")
+        prefix(2)
+        filled(0, 3)
+        compare(3)
+        votes(3, "psE")
+        mm(psS, T.NI[:], T.S16[:], True, False, ["NI", "S16"], ["psS"])
+        mm(psS, ones, row, False, False, ["ob", "row"], ["psS"])
+
+        won(0, 192, "psV")
+        runs(0, 192)
+        klist(0, 12)
+        high(0, 12)
+        prefix(3)
+        filled(3, 4)
+        scan(T.CH[:, 0:192], T.ob[:, 0:192], T.HF[:, 0:192], OP.mult, OP.add, ["ob", ("HF", 0, 192)], [("CH", 0, 192)])
+        count(0, 192, "acca")
+        won(192, 256, "psE")
+        runs(192, 256)
+        tt(T.kb[:], T.st[:, 15:256:16], T.KB[:], OP.add, ["st", "KB"], ["kb"])
+        klist(12, 16)
+        high(12, 16)
+        cp(T.kl1[:], T.kb[:], ["kb"], ["kl1"])
+        do("v", lambda v: v.tensor_reduce(T.krr[:], T.st[:, 15:256:16], AxisListType.X, OP.add), ["st"], ["krr"])
+        act(T.K[:], T.KT[:, 0:16].indirect(T.kl0[:, 0:16]), AF.Copy, ["KT", "kl0"], ["K"])
+        tt(T.D[:], T.PM[:, 0:NB].indirect(T.kl1[:, 0:16]), T.P[:, 0:NB:16], OP.subtract, ["PM", "kl1", "P"], ["D"])
+        act(T.Y[:, 0:256], T.D[:], AF.Abs, ["D"], [("Y", 0, 256)])
+        ts(T.BA[:], T.BO[:], T.krr[:], 16.0, OP.mult, OP.mult, ["BO", "krr"], ["BA"])
+        mm(psD, T.BA[:], T.ob[:], False, True, ["BA", "ob"], ["psD"])
+        for q in range(16):
+            mm(psL, T.WE[:, 15 - q:143 - q], T.Y[:, q:256:16], False, False, ["WE", ("Y", 0, 256)], ["psL"])
+        mm(psL, T.BA[:], T.o256[:, 0:16], False, True, ["BA", "o256"], ["psL"])
+        for b in ("psR", "psS"):
+            mm(T[b][:, 0:256], T.BA[:], T.o256[:], False, False, ["BA", "o256"], [b])
+            mm(T[b][:, 0:256], T.WB[:], T.Y[:, 0:256], False, True, ["WB", ("Y", 0, 256)], [b])
+
+        scan(T.CH[:, 192:256], T.ob[:, 192:256], T.HF[:, 192:256], OP.mult, OP.add, ["ob", ("HF", 192, 256), ("CH", 191, 192)],
+             [("CH", 192, 256)], ini=T.CH[:, 191:192])
+        count(192, 256, "accb")
+        ts(T.accp[:], T.acca[:], -0.5, 128.0, OP.mult, OP.add, ["acca"], ["accp"])
+        ts(T.ZF[:], T.K[:], 8.0, None, OP.is_lt, None, ["K"], ["ZF"])
+        ts(T.C[:], T.K[:], T.d16[:], None, OP.is_gt, None, ["K", "d16"], ["C"])
+        scan(T.CZ[:], T.ob[:], T.ZF[:], OP.mult, OP.add, ["ob", "ZF"], ["CZ"])
+        for c in range(2):
+            ts(T.hl[:, c:c + 1], T.accb[:, c:c + 1], -0.5, T.accp[:, c:c + 1], OP.mult, OP.add, ["accb", "accp"], [("hl", c, c + 1)])
+        act(T[PKn][:], T.Y[:, 0:272].indirect(T.hl[:, 0:2]), AF.Copy, ["Y", "hl"], [PKn])
+        send(dst, T[PKn][:], T[RXn][:], [PKn], "arr%d" % t)
+        landed(frm, "arr%d" % t, RXn)
+        for c in range(2):
+            act(T["J%d" % c][:], T.CZ[:], AF.Sign, ["CZ", "bs"], ["J%d" % c, ("accz", c, c + 1)], bias=T.bs[:, c:c + 1],
+                accum_out=T.accz[:, c:c + 1])
+        act(T.EK[:], T.ET[:, 0:16].indirect(T.kl0[:, 0:16]), AF.Copy, ["ET", "kl0"], ["EK"])
+
+        tt(psD, psD, T.C[:], OP.mult, ["psD", "C"], ["psD"])
+        ts(T.nk[:], T.nc[:], T.CZ[:, 255:256], None, OP.is_ge, None, ["nc", "CZ"], ["nk"])
+        tt(psD, psD, T.S16[:], OP.add, ["psD", "S16"], ["psD"])
+        cp(T.VI[:], psL, ["psL"], ["VI"])
+        tt(T.nd[:], T.nk[:], T.dm[:], OP.mult, ["nk", "dm"], ["nd"])
+        ts(T.VB[:], T.VI[:], 4, 4095, OP.arith_shift_right, OP.bitwise_and, ["VI"], ["VB"])
+        ts(T.zl[:], T.accz[:], -0.5, 128.0, OP.mult, OP.add, ["accz"], ["zl"])
+        cp(T.VL[:], T.VB[:], ["VB"], ["VL"])
+        act(T.OW[:], T.Y[:, 0:272].indirect(T.zl[:, 0:2]), AF.Identity, ["Y", "zl"], ["OW"], bias=-256.0)
+        act(T.vraw[:, 0:256], psR, AF.Copy, ["psR"], [("vraw", 0, 256)])
+        act(T.G32[:], T.vraw[:, 0:272].indirect(T.zl[:, 0:2]), AF.Copy, ["vraw", "zl"], ["G32"])
+        cp(spare.indirect(T.VL[:, 0:16]), T.Y[:, 0:256], ["VL", ("Y", 0, 256)], ["B"])
+
+        tt(T.t3[:], psS, T.EK[:], OP.mult, ["psS", "EK"], ["t3"])
+        tt(T.GM[:], T.G32[:], T.DM[:], OP.mult, ["G32", "DM"], ["GM"])
+        for c in range(2):
+            act(T["J%d" % c][:, 0:16], T.GM[:, 16 * c:16 * c + 16], AF.Copy, ["GM"], ["J%d" % c, ("rd", c, c + 1)],
+                accum_out=T.rd[:, c:c + 1])
+        tt(T.UI[:], psD, T.t3[:], OP.add, ["psD", "t3"], ["UI"])
+        cp(T.ri[:], T.rd[:], ["rd"], ["ri"])
+        ts(T.SI[:], T.UI[:], 4, 4095, OP.arith_shift_right, OP.bitwise_and, ["UI"], ["SI"])
+        ts(T.rb[:], T.ri[:], 4, 4095, OP.arith_shift_right, OP.bitwise_and, ["ri"], ["rb"])
         if last:
-            arrivals()
-            dma("y", "out_yb", T.yb[:], T.B[:, 0:NB], [("B", 0, NB)], [])
-            stacks()
+            cp(T.yof[:], T.SI[:], ["SI"], ["yof"])
             dma("s", "out_yo", T.yo[:], T.yof[:], ["yof"], [])
         else:
-            stacks()
-            arrivals()
+            cp(T.SU[:], T.SI[:], ["SI"], ["SU"])
+        for c in range(2):
+            ts(T.OL[:, c:c + 1], T.rb[:, c:c + 1], T.nd[:, c:c + 1], None, OP.max, None, ["rb", "nd"], [("OL", c, c + 1)])
+        if not last:
+            factors()
+        tt(T.u[:], T[RXn][:], T.OW[:], OP.max, [RXn, "OW"], ["u"])
+        ts(T.w[:], T.u[:], 0.0, 256.0, OP.is_lt, OP.mult, ["u"], ["w"])
+        tt(spare.indirect(T.OL[:, 0:2]), T.u[:], T.w[:], OP.add, ["OL", "u", "w"], ["B"])
 
+    dma("y", "out_yb", T.yb[:], balls, [("B", 0, NB)], [])
     for sem in sorted(total):
         wait_for("g", sem, total[sem], {})

import numpy as np
from concourse.mybir import AluOpType, AxisListType, ActivationFunctionType

OP = AluOpType
AF = ActivationFunctionType
ROUNDS = 3
NB = 4096
DUMP = 32
CH = 4
CW = NB // CH
REP = 4

SCRATCH = {}


def _declare(where, dtype, **shapes):
    for name, n in shapes.items():
        SCRATCH[name] = (where, [128] + (n if isinstance(n, list) else [n]), dtype)


_declare("sbuf", "bfloat16", B=NB + DUMP, P=NB, PM=NB, pat=64, WN=[16, 256], tw=256, st=256, K=256, D=256, Y=272, HF=256,
         ZF=256, CH=256, CZ=256, J0=256, J1=256, C=256, EK=256, ob=256, o256=256, r57=256, ID=128, B1=128, BO=128, BA=128,
         WB=128, E1=144, E2=144, E01=144, WE=144, RS=CW, KS=256, KT=16, HT=16, ET=16, iL=16, row=256, wb=1, OW=32, u=32,
         w=32, PK0=32, PK1=32, PK2=32, RX0=32, RX1=32, RX2=32)
_declare("sbuf", "float32", S16=256, kb=16, krr=1, acca=2, accb=2, accp=2, accz=2, vraw=272, G32=32, GM=32, rd=2, nk=2,
         nd=2, ef=256, zu=256, t3=256, yof=256, of32=128, c16=128, cm1=128, LE=128, LS=128, NI=128, rc=1, d16=1, bs=2,
         nc=2, dm=2, j16=16, iF=16, KB=16, rowf=256, cm=32, DM=32, wf=1)
_declare("sbuf", "int32", SI=256, eI=256, UI=256, VI=16, VB=16, ri=2, rb=2, pI=1, rI=1, wI=1, wA=1)
_declare("sbuf", "uint16", SU=256, kl0=16, kl1=16, hl=2, zl=2, OL=2, VL=16)
_declare("psum", "float32", psX0=512, psX1=512, psV=512, psE=512, psD=512, psS=512, psR=512, psL=512)

DMAS = ["in_stk", "in_wt", "in_ball", "out_yo", "out_yb"]
SEMAPHORES = ["qv", "qs", "qt", "qg", "ls"] + ["dma_" + d for d in DMAS] + ["arr%d" % t for t in range(ROUNDS)]


def rank_program(g, core, T, topo):
    rank = T.rank_of(core)
    if rank is None:
        return
    queues = {"g": g, "v": g.vector, "s": g.scalar, "t": g.tensor, "y": g.sync}
    qsem = {"g": "qg", "v": "qv", "s": "qs", "t": "qt"}
    total = {}
    know = dict((q, {}) for q in queues)
    hist = {}

    def wait_for(q, sem, val, clock):
        if know[q].get(sem, 0) >= val:
            return
        queues[q].wait_ge(T.sem[sem], val)
        know[q][sem] = val
        for s2, v2 in clock.items():
            if know[q].get(s2, 0) < v2:
                know[q][s2] = v2

    def need(q, reads, writes, waw=True):
        deps = []
        for acc, isw in ((reads, False), (writes, True)):
            for (b, lo, hi) in acc:
                for h in hist.get(b, ()):
                    same = h[3] == q
                    if b.startswith("ps") and not same:
                        deps.append(h)
                        continue
                    if h[1] <= lo or hi <= h[0] or not (isw or h[2]):
                        continue
                    if same and (q == "t" or (isw and (not h[2] or not waw))):
                        continue
                    deps.append(h)
        for h in sorted(deps, key=lambda h: -h[5]):
            wait_for(q, h[4], h[5], h[6])

    def note(q, sem, val, reads, writes):
        clock = dict(know.get(q, {}))
        clock[sem] = max(clock.get(sem, 0), val)
        for acc, isw in ((reads, False), (writes, True)):
            for (b, lo, hi) in acc:
                old = hist.get(b, [])
                if isw and b.startswith("ps"):
                    old = []
                elif isw:
                    old = [h for h in old if not (lo <= h[0] and h[1] <= hi)]
                else:
                    old = [h for h in old if not (h[3] == q and not h[2] and lo <= h[0] and h[1] <= hi)]
                hist[b] = old + [(lo, hi, isw, q, sem, val, clock)]

    def reg(r):
        return r if isinstance(r, tuple) else (r, 0, int(np.prod(SCRATCH[r][1][1:])))

    def do(q, call, reads, writes, waw=True):
        R, W = [reg(r) for r in reads], [reg(w) for w in writes]
        need(q, R, W, waw)
        sem = qsem[q]
        total[sem] = total.get(sem, 0) + 1
        call(queues[q]).then_inc(T.sem[sem], 1)
        note(q, sem, total[sem], R, W)

    def dma(q, name, out, in_, reads, writes):
        R, W = [reg(r) for r in reads], [reg(w) for w in writes]
        need(q, R, W)
        sem = "dma_" + name
        total[sem] = 16
        queues[q].dma_start(out, in_).then_inc(T.sem[sem], 16)
        note(sem, sem, 16, R, W)

    def lanes_of(src, dst):
        return topo.engines(src, dst)[:8]

    def send(dst, src, out, reads, sem):
        need("g", [reg(r) for r in reads], [])
        rid, pid, _ = topo.addr(dst)
        eng = lanes_of(core, dst)
        total["ls"] = total.get("ls", 0) + len(eng)
        g.remote_dma(out, src, T.sem[sem], T.sem["ls"], pid, rid, sum(1 << e for e in eng))

    def landed(frm, sem, name):
        total[sem] = len(lanes_of(frm, core))
        note("remote", sem, total[sem], [], [reg(name)])

    def ts(out, in0, s1, s2, op0, op1, R, W):
        ops = (op0,) if op1 is None else (op0, op1)
        do("v", lambda v: v.tensor_scalar(out, in0, s1, s2, *ops), R, W)

    def tt(out, a, b, op, R, W, waw=True):
        do("v", lambda v: v.tensor_tensor(out, a, b, op), R, W, waw)

    def cp(out, a, R, W):
        do("v", lambda v: v.tensor_copy(out, a), R, W)

    def ms(out, c, W):
        do("v", lambda v: v.memset(out, c), [], W)

    def scan(out, d0, d1, o0, o1, R, W, ini=0.0):
        do("v", lambda v: v.tensor_tensor_scan(out, d0, d1, ini, o0, o1), R, W)

    def act(out, a, f, R, W, **kw):
        do("s", lambda s: s.activation(out, a, f, **kw), R, W)

    def mm(out, l, r, start, stop, R, W):
        do("t", lambda x: x.matmul(out, l, r, start, stop), R, W)

    def asel(out, a, pat, cmp, fill, base, mult, R, W):
        do("g", lambda x: x.affine_select(out, a, pat, cmp, fill, base, mult), R, W)

    def iota(out, pat, base, mult, W, **kw):
        do("g", lambda x: x.iota(out, pat, base, mult, **kw), [], W)

    small = {"allow_small_or_imprecise_dtypes": True}

    dma("y", "in_stk", T.SI[:], T.stk[:], [], ["SI"])
    dma("s", "in_ball", T.B[:, 0:NB], T.ball[:], [], [("B", 0, NB)])
    dma("y", "in_wt", T.wb[:], T.wt[:], [], ["wb"])

    iota(T.pI[:], [[0, 1]], 0, 1, ["pI"])
    ms(T.of32[:], 1.0, ["of32"])
    ms(T.cm1[:], -1.0, ["cm1"])
    ms(T.ob[:], 1.0, ["ob"])
    ms(T.c16[:], 0.0625, ["c16"])
    blk = [[-16, 8], [0, 16]]
    asel(T.LE[:], T.of32[:], blk, OP.is_equal, 0.0, 0, 1, ["of32"], ["LE"])
    asel(T.ID[:], T.ob[:, 0:128], [[-1, 128]], OP.is_equal, 0.0, 0, 1, ["ob"], ["ID"])
    asel(T.NI[:], T.cm1[:], [[-1, 128]], OP.is_equal, 0.0, 0, 1, ["cm1"], ["NI"])
    iota(T.rowf[:], [[16, 256]], 0, 0, ["rowf"], **small)
    iota(T.j16[:], [[16, 16]], 0, 0, ["j16"], **small)
    iota(T.cm[:], [[0, 2], [1, 16]], 0, 0, ["cm"], **small)
    iota(T.KT[:], [[16, 16]], 0, 0, ["KT"], **small)
    asel(T.E1[:], T.ob[:, 0:144], [[-16, 9], [0, 16]], OP.is_ge, 0.0, 0, 1, ["ob"], ["E1"])
    asel(T.E2[:], T.E1[:], [[16, 9], [0, 16]], OP.is_ge, 0.0, 15, -1, ["E1"], ["E2"])
    asel(T.E01[:], T.E2[:], [[0, 9], [1, 16]], OP.is_equal, 0.0, -15, 0, ["E2"], ["E01"])
    asel(T.LS[:], T.c16[:], [[-1, 128]], OP.is_equal, 0.0, -1, 1, ["c16"], ["LS"])
    asel(T.B1[:], T.ob[:, 0:128], blk, OP.is_ge, 0.0, 0, 1, ["ob"], ["B1"])
    asel(T.BO[:], T.B1[:], [[16, 8], [0, 16]], OP.is_ge, 0.0, 15, -1, ["B1"], ["BO"])

    ms(T.pat[:], 0.0, ["pat"])
    ms(T.RS[:], 1.0, ["RS"])
    ms(T.r57[:], 57344.0, ["r57"])
    ms(T.RS[:, 1:CW:16], 0.0, ["RS"])
    ms(T.KS[:], -1.0, ["KS"])
    ms(T.pat[:, 0:64:16], 16.0, ["pat"])
    ms(T.o256[:], 256.0, ["o256"])
    ms(T.KS[:, 0:256:16], 100.0, ["KS"])
    ms(T.B[:, NB:NB + DUMP], 0.0, [("B", NB, NB + DUMP)])
    ms(T.Y[:, 256:272], -512.0, [("Y", 256, 272)])
    ms(T.vraw[:, 256:272], 0.0, [("vraw", 256, 272)])
    cp(T.SU[:], T.SI[:], ["SI"], ["SU"])

    def early_constants():
        ts(T.rI[:], T.pI[:], 15, None, OP.bitwise_and, None, ["pI"], ["rI"])
        cp(T.row[:], T.rowf[:], ["rowf"], ["row"])
        cp(T.rc[:], T.rI[:], ["rI"], ["rc"])
        ts(T.HT[:], T.KT[:], 160.0, None, OP.is_ge, None, ["KT"], ["HT"])
        ts(T.iF[:], T.j16[:], T.rc[:], None, OP.add, None, ["j16", "rc"], ["iF"])
        ts(T.d16[:], T.rc[:], 16.0, None, OP.mult, None, ["rc"], ["d16"])
        ts(T.nc[:, 0:1], T.rc[:], 0.0, None, OP.add, None, ["rc"], [("nc", 0, 1)])
        ts(T.nc[:, 1:2], T.rc[:], 16.0, None, OP.add, None, ["rc"], [("nc", 1, 2)])
        ts(T.KB[:], T.iF[:], 16.0, 14.0, OP.mult, OP.add, ["iF"], ["KB"])
        ts(T.ET[:], T.KT[:], T.d16[:], None, OP.is_equal, None, ["KT", "d16"], ["ET"])
        ts(T.iL[:], T.iF[:], 16.0, None, OP.mult, None, ["iF"], ["iL"])
        ts(T.DM[:], T.cm[:], T.rc[:], None, OP.is_equal, None, ["cm", "rc"], ["DM"])
        ts(T.bs[:], T.nc[:], -1.0, -0.5, OP.mult, OP.add, ["nc"], ["bs"])
        ts(T.dm[:], T.nc[:], float(NB), None, OP.add, None, ["nc"], ["dm"])
        cp(T.wI[:], T.wb[:], ["wb"], ["wI"])
        ts(T.wA[:], T.wI[:], 15, None, OP.bitwise_and, None, ["wI"], ["wA"])
        ts(T.wf[:], T.wA[:], 4096.0, None, OP.mult, None, ["wA"], ["wf"])

    def late_constants():
        ts(T.WE[:], T.E01[:], T.wf[:], None, OP.mult, None, ["E01", "wf"], ["WE"])
        ts(T.WB[:], T.BO[:], T.wf[:], None, OP.mult, None, ["BO", "wf"], ["WB"])

    balls, spare = T.B[:, 0:NB], T.B[:, 0:NB + DUMP]
    ones, row = T.ob[0:1, 0:128], T.row[0:1, :]
    psD, psS, psR, psL = T.psD[:, 0:256], T.psS[:, 0:256], T.psR[:, 0:256], T.psL[:, 0:16]

    def factors():
        ts(T.eI[:], T.SI[:], 1023, None, OP.bitwise_and, None, ["SI"], ["eI"])
        ts(T.S16[:], T.SI[:], 16.0, None, OP.mult, None, ["SI"], ["S16"])
        ts(T.ef[:], T.eI[:], 2.0, 1.0, OP.mult, OP.add, ["eI"], ["ef"])
        mm(T.psE[:, 0:256], T.LE[:], T.ef[:], True, True, ["LE", "ef"], ["psE"])

    factors()
    early_constants()

    for t in range(ROUNDS):
        last = t == ROUNDS - 1
        n = len(T.cores)
        dst, frm = T.cores[(rank + t + 1) % n], T.cores[(rank - t - 1) % n]
        PKn, RXn = "PK%d" % t, "RX%d" % t

        def part(name, c):
            return (name, CW * c, CW * c + CW)

        def gather(q, a, b):
            out, off = T.P[:, 16 * a:16 * b], T.SU[:, a:b]
            R, W = [("B", 0, NB), ("SU", a, b)], [("P", 16 * a, 16 * b)]
            if q == "s":
                act(out, balls.indirect(off), AF.Copy, R, W)
            else:
                cp(out, balls.indirect(off), R, W)

        def tops(c):
            b = "psX%d" % (c % 2)
            for r in range(REP):
                mm(T[b][:, r:64 * REP:REP], T.ID[:], T.P[:, CW * c:CW * c + CW:16], True, True, ["ID", part("P", c)], [b])

        def compare(c):
            b, s = "psX%d" % (c % 2), 16 // REP
            for d in range(s):
                tt(T.WN[:, 4 * c:4 * c + 4, d:256:s], T.P[:, CW * c + d:CW * c + CW:s], T[b][:, 0:64 * REP],
                   OP.is_lt, [part("P", c), b], [part("WN", c)], waw=False)

        def votes(c, b):
            mm(T[b][:, 64 * c:64 * c + 64], ones, T.pat[0:1, :], True, False, ["ob", "pat"], [b])
            for q in range(16):
                mm(T[b][:, 64 * c:64 * c + 64], T.E01[:, 15 - q:143 - q], T.WN[:, 4 * c:4 * c + 4, 16 * q:16 * q + 16],
                   False, q == 15, ["E01", part("WN", c)], [b])

        def prefix(c):
            scan(T.PM[:, CW * c:CW * c + CW], T.RS[:], T.P[:, CW * c:CW * c + CW], OP.mult, OP.max,
                 ["RS", part("P", c)], [part("PM", c)])

        def filled(c, e):
            a, e = CW * c, CW * e
            act(T.PM[:, a:e:16], T.P[:, a:e:16], AF.Identity, [("P", a, e)], [("PM", a, e)], bias=255.0, scale=0.0)

        def won(a, e, b):
            ts(T.tw[:, a:e], T[b][:, a:e], 9.0, 16.0, OP.is_ge, OP.mult, [b], [("tw", a, e)])

        def runs(a, e):
            scan(T.st[:, a:e], T.KS[:, a:e], T.tw[:, a:e], OP.add, OP.min, ["KS", ("tw", a, e)], [("st", a, e)])

        def klist(j, e):
            ts(T.kl0[:, j:e], T.st[:, 16 * j + 15:16 * e:16], 14.0, None, OP.add, None, [("st", 16 * j, 16 * e)], [("kl0", j, e)])

        def high(j, e):
            act(T.HF[:, 16 * j:16 * e], T.HT[:, 0:16].indirect(T.kl0[:, j:e]), AF.Copy, ["HT", ("kl0", j, e)], [("HF", 16 * j, 16 * e)])

        def count(a, e, acc):
            for c in range(2):
                act(T["J%d" % c][:, a:e], T.CH[:, a:e], AF.Sign, [("CH", a, e), "bs"], ["J%d" % c, (acc, c, c + 1)],
                    bias=T.bs[:, c:c + 1], accum_out=T[acc][:, c:c + 1])

        gather("s", 0, 32)
        gather("v", 32, 64)
        gather("s", 64, 128)
        gather("s", 128, 192)
        gather("s", 192, 256)
        tops(0)
        compare(0)
        mm(psD, T.NI[:], T.S16[:], True, False, ["NI", "S16"], ["psD"])
        mm(psD, ones, T.r57[0:1, :], False, False, ["ob", "r57"], ["psD"])
        mm(psR, ones, row, True, False, ["ob", "row"], ["psR"])
        mm(psL, T.ID[:], T.iL[:], True, False, ["ID", "iL"], ["psL"])
        tops(1)
        votes(0, "psV")
        tt(T.zu[:], T.S16[:], T.psE[:, 0:256], OP.mult, ["S16", "psE"], ["zu"])
        tops(2)
        prefix(0)
        compare(1)
        votes(1, "psV")
        mm(psD, T.LS[:], T.zu[:], False, False, ["LS", "zu"], ["psD"])
        if t == 0:
            late_constants()
        tops(3)
        prefix(1)
        compare(2)
        votes(2, "psV")
        prefix(2)
        filled(0, 3)
        compare(3)
        votes(3, "psE")
        mm(psS, T.NI[:], T.S16[:], True, False, ["NI", "S16"], ["psS"])
        mm(psS, ones, row, False, False, ["ob", "row"], ["psS"])

        won(0, 192, "psV")
        runs(0, 192)
        klist(0, 12)
        high(0, 12)
        prefix(3)
        filled(3, 4)
        scan(T.CH[:, 0:192], T.ob[:, 0:192], T.HF[:, 0:192], OP.mult, OP.add, ["ob", ("HF", 0, 192)], [("CH", 0, 192)])
        count(0, 192, "acca")
        won(192, 256, "psE")
        runs(192, 256)
        tt(T.kb[:], T.st[:, 15:256:16], T.KB[:], OP.add, ["st", "KB"], ["kb"])
        klist(12, 16)
        high(12, 16)
        cp(T.kl1[:], T.kb[:], ["kb"], ["kl1"])
        do("v", lambda v: v.tensor_reduce(T.krr[:], T.st[:, 15:256:16], AxisListType.X, OP.add), ["st"], ["krr"])
        act(T.K[:], T.KT[:, 0:16].indirect(T.kl0[:, 0:16]), AF.Copy, ["KT", "kl0"], ["K"])
        tt(T.D[:], T.PM[:, 0:NB].indirect(T.kl1[:, 0:16]), T.P[:, 0:NB:16], OP.subtract, ["PM", "kl1", "P"], ["D"])
        act(T.Y[:, 0:256], T.D[:], AF.Abs, ["D"], [("Y", 0, 256)])
        ts(T.BA[:], T.BO[:], T.krr[:], 16.0, OP.mult, OP.mult, ["BO", "krr"], ["BA"])
        mm(psD, T.BA[:], T.ob[:], False, True, ["BA", "ob"], ["psD"])
        for q in range(16):
            mm(psL, T.WE[:, 15 - q:143 - q], T.Y[:, q:256:16], False, False, ["WE", ("Y", 0, 256)], ["psL"])
        mm(psL, T.BA[:], T.o256[:, 0:16], False, True, ["BA", "o256"], ["psL"])
        for b in ("psR", "psS"):
            mm(T[b][:, 0:256], T.BA[:], T.o256[:], False, False, ["BA", "o256"], [b])
            mm(T[b][:, 0:256], T.WB[:], T.Y[:, 0:256], False, True, ["WB", ("Y", 0, 256)], [b])

        scan(T.CH[:, 192:256], T.ob[:, 192:256], T.HF[:, 192:256], OP.mult, OP.add, ["ob", ("HF", 192, 256), ("CH", 191, 192)],
             [("CH", 192, 256)], ini=T.CH[:, 191:192])
        count(192, 256, "accb")
        ts(T.accp[:], T.acca[:], -0.5, 128.0, OP.mult, OP.add, ["acca"], ["accp"])
        ts(T.ZF[:], T.K[:], 8.0, None, OP.is_lt, None, ["K"], ["ZF"])
        ts(T.C[:], T.K[:], T.d16[:], None, OP.is_gt, None, ["K", "d16"], ["C"])
        scan(T.CZ[:], T.ob[:], T.ZF[:], OP.mult, OP.add, ["ob", "ZF"], ["CZ"])
        for c in range(2):
            ts(T.hl[:, c:c + 1], T.accb[:, c:c + 1], -0.5, T.accp[:, c:c + 1], OP.mult, OP.add, ["accb", "accp"], [("hl", c, c + 1)])
        act(T[PKn][:], T.Y[:, 0:272].indirect(T.hl[:, 0:2]), AF.Copy, ["Y", "hl"], [PKn])
        send(dst, T[PKn][:], T[RXn][:], [PKn], "arr%d" % t)
        landed(frm, "arr%d" % t, RXn)
        for c in range(2):
            act(T["J%d" % c][:], T.CZ[:], AF.Sign, ["CZ", "bs"], ["J%d" % c, ("accz", c, c + 1)], bias=T.bs[:, c:c + 1],
                accum_out=T.accz[:, c:c + 1])
        act(T.EK[:], T.ET[:, 0:16].indirect(T.kl0[:, 0:16]), AF.Copy, ["ET", "kl0"], ["EK"])

        tt(psD, psD, T.C[:], OP.mult, ["psD", "C"], ["psD"])
        ts(T.nk[:], T.nc[:], T.CZ[:, 255:256], None, OP.is_ge, None, ["nc", "CZ"], ["nk"])
        tt(psD, psD, T.S16[:], OP.add, ["psD", "S16"], ["psD"])
        cp(T.VI[:], psL, ["psL"], ["VI"])
        tt(T.nd[:], T.nk[:], T.dm[:], OP.mult, ["nk", "dm"], ["nd"])
        ts(T.VB[:], T.VI[:], 4, 4095, OP.arith_shift_right, OP.bitwise_and, ["VI"], ["VB"])
        ts(T.zl[:], T.accz[:], -0.5, 128.0, OP.mult, OP.add, ["accz"], ["zl"])
        cp(T.VL[:], T.VB[:], ["VB"], ["VL"])
        act(T.OW[:], T.Y[:, 0:272].indirect(T.zl[:, 0:2]), AF.Identity, ["Y", "zl"], ["OW"], bias=-256.0)
        act(T.vraw[:, 0:256], psR, AF.Copy, ["psR"], [("vraw", 0, 256)])
        act(T.G32[:], T.vraw[:, 0:272].indirect(T.zl[:, 0:2]), AF.Copy, ["vraw", "zl"], ["G32"])
        cp(spare.indirect(T.VL[:, 0:16]), T.Y[:, 0:256], ["VL", ("Y", 0, 256)], ["B"])

        tt(T.t3[:], psS, T.EK[:], OP.mult, ["psS", "EK"], ["t3"])
        tt(T.GM[:], T.G32[:], T.DM[:], OP.mult, ["G32", "DM"], ["GM"])
        for c in range(2):
            act(T["J%d" % c][:, 0:16], T.GM[:, 16 * c:16 * c + 16], AF.Copy, ["GM"], ["J%d" % c, ("rd", c, c + 1)],
                accum_out=T.rd[:, c:c + 1])
        tt(T.UI[:], psD, T.t3[:], OP.add, ["psD", "t3"], ["UI"])
        cp(T.ri[:], T.rd[:], ["rd"], ["ri"])
        ts(T.SI[:], T.UI[:], 4, 4095, OP.arith_shift_right, OP.bitwise_and, ["UI"], ["SI"])
        ts(T.rb[:], T.ri[:], 4, 4095, OP.arith_shift_right, OP.bitwise_and, ["ri"], ["rb"])
        if last:
            cp(T.yof[:], T.SI[:], ["SI"], ["yof"])
            dma("s", "out_yo", T.yo[:], T.yof[:], ["yof"], [])
        else:
            cp(T.SU[:], T.SI[:], ["SI"], ["SU"])
        for c in range(2):
            ts(T.OL[:, c:c + 1], T.rb[:, c:c + 1], T.nd[:, c:c + 1], None, OP.max, None, ["rb", "nd"], [("OL", c, c + 1)])
        if not last:
            factors()
        tt(T.u[:], T[RXn][:], T.OW[:], OP.max, [RXn, "OW"], ["u"])
        ts(T.w[:], T.u[:], 0.0, 256.0, OP.is_lt, OP.mult, ["u"], ["w"])
        tt(spare.indirect(T.OL[:, 0:2]), T.u[:], T.w[:], OP.add, ["OL", "u", "w"], ["B"])

    dma("y", "out_yb", T.yb[:], balls, [("B", 0, NB)], [])
    for sem in sorted(total):
        wait_for("g", sem, total[sem], {})
